import numpy as np
import ml_dtypes


def mxq(x, axis, fmt="e4m3"):
    dtype, down = {"e4m3": (ml_dtypes.float8_e4m3fn, 7), "e5m2": (ml_dtypes.float8_e5m2, 14)}[fmt]
    v = np.moveaxis(np.asarray(x, np.float32).astype(ml_dtypes.bfloat16).astype(np.float64), axis, -1)
    blocks = v.reshape(v.shape[:-1] + (-1, 32))
    amax = np.abs(blocks).max(-1, keepdims=True)
    byte = np.maximum(np.where(amax > 0, np.frexp(amax)[1] - 1 + 127, 0) - down, 1)
    scale = np.exp2(byte - 127.0)
    codes = (blocks / scale).astype(np.float32).astype(dtype).astype(np.float64)
    return np.moveaxis((codes * scale).reshape(v.shape), -1, axis)


WIDE = False


def mx_kscale(k):
    if not WIDE:
        return np.ones(k)
    levels = np.array([10, -10, 5, -5, 0])
    if k % 512:
        return np.exp2(np.random.permutation(np.resize(levels, k // 32))).repeat(32)
    a = np.empty((k // 512, 16))
    for p in range(k // 512):
        a[p, :8] = np.random.permutation(np.resize(levels, 8))
        for g in range(8):
            far = levels[np.abs(levels - a[p, g]) >= 10]
            a[p, g + 8] = far[np.random.randint(len(far))]
    return np.exp2(a.ravel()).repeat(32)


def f64(x):
    return np.asarray(x).astype(np.float64)


def striped(idx):
    return np.tile(idx.reshape(-1, 16).T, (8, 1)).astype(np.uint16)


def unstriped(offs):
    return offs[:16].T.reshape(-1).astype(np.int64)


def striped8(idx):
    return np.concatenate([x.reshape(-1, 16).T for x in idx]).astype(np.uint16)


def runs(offs, k):
    lists = np.stack([offs[16 * r : 16 * r + 16].T.reshape(-1) for r in range(8)]).astype(np.int64)
    return lists[np.arange(k) % 512 // 64]


def pack_weight(w):
    k, n = w.shape
    w = f64(np.asarray(w, np.float32).astype(ml_dtypes.bfloat16)).reshape(k // 32, 32, n)
    amax = np.abs(w).max(1)
    byte = np.clip(np.where(amax > 0, np.frexp(amax)[1] - 1 + 127 - 7, 1), 1, 254)
    scaled = (w * np.exp2(127.0 - byte)[:, None, :]).reshape(k, n).astype(np.float32)
    words = np.ascontiguousarray(scaled.reshape(k // 512, 128, 4, n).transpose(0, 1, 3, 2)).astype(ml_dtypes.float8_e4m3fn).view(np.uint8)
    return words, np.ascontiguousarray(byte.astype(np.uint8).reshape(k // 512, 16, n))


def unpack_weight(words, scales):
    g, p, n, _ = words.shape
    vals = np.ascontiguousarray(words).view(ml_dtypes.float8_e4m3fn).astype(np.float64) * np.repeat(np.exp2(scales.astype(np.float64) - 127.0), 8, axis=1)[..., None]
    return vals.transpose(0, 1, 3, 2).reshape(g * 512, n)


def relu(v):
    return np.maximum(v, 0.0)

def planes(y):
    n, m = y.shape
    v = y.astype(np.float32).astype(ml_dtypes.bfloat16).astype(np.float64).reshape(n // 32, 32, m)
    top = np.abs(v).max(1)
    byte = np.clip(np.where(top > 0, np.frexp(top)[1] - 1 + 127 - 7, 1), 1, 254)
    codes = (v * np.exp2(127.0 - byte)[:, None, :]).reshape(n, m).astype(np.float32).astype(ml_dtypes.float8_e4m3fn).view(np.uint8)
    words = codes.reshape(n // 512, 128, 4, m).transpose(0, 1, 3, 2)
    return np.ascontiguousarray(words), np.ascontiguousarray(byte.astype(np.uint8).reshape(n // 512, 16, m))


K, T, S, N, H = 512, 2048, 512, 512, 512


def setup_inputs():
    n = np.random.standard_normal
    s = mx_kscale(K)[:, None]
    u = mx_kscale(H)
    packed_xT = pack_weight(n((K, T)) * s)
    packed_w3 = pack_weight(n((H, N)) / np.sqrt(H) / u[:, None])
    return {
        "x_words": packed_xT[0],
        "x_scales": packed_xT[1],
        "w1": (n((K, H)) / np.sqrt(K) / s * u).astype(np.float32),
        "w2": (n((H, H)) / np.sqrt(H) / u[:, None] * u).astype(np.float32),
        "w3_words": packed_w3[0],
        "w3_scales": packed_w3[1],
        "res": n((N, S)).astype(np.float32),
        "offs": striped(np.random.permutation(T)[:S]),
        "n1": striped8(np.stack([np.random.permutation(S) for _ in range(8)])),
        "n2": striped8(np.stack([np.random.permutation(S) for _ in range(8)])),
        "dst": striped8(np.stack([np.random.permutation(S) for _ in range(8)])),
    }


def reference(x_words, x_scales, w1, w2, w3_words, w3_scales, res, offs, n1, n2, dst):
    xq = unpack_weight(x_words, x_scales)[:, unstriped(offs)]
    y = mxq(f64(w1), 0, "e4m3").T @ xq
    z = y - (np.maximum(y[np.arange(H)[:, None], runs(n1, H)], y[np.arange(H)[:, None], runs(n2, H)]))
    h = mxq(f64(w2), 0, "e4m3").T @ mxq(z, 0, "e4m3")
    hr = relu(h)
    hs = np.zeros((H, S))
    hs[np.arange(H)[:, None], runs(dst, H)] = hr
    z2 = hs - y
    out_0 = f64(res) + (unpack_weight(w3_words, w3_scales).T @ mxq(z2, 0, "e4m3"))
    return (out_0,) + planes(out_0)

@@ -1,0 +1,213 @@
+from contextlib import ExitStack
+
+import concourse.mybir as mybir
+
+K, T, S, N, H = 512, 2048, 512, 512, 512
+FLOPS = 2 * S * (K * H + H * H + H * N)
+
+F32 = mybir.dt.float32
+BF16 = mybir.dt.bfloat16
+I32 = mybir.dt.int32
+U32 = mybir.dt.uint32
+U16 = mybir.dt.uint16
+U8 = mybir.dt.uint8
+FP8X4 = mybir.dt.float8_e4m3fn_x4
+ALU = mybir.AluOpType
+ACT = mybir.ActivationFunctionType
+
+P = 128
+PACK = 4
+HALF = S // 2
+LIST_COLS = HALF // 16
+BLOCK = 128
+W_VEC = 40
+
+
+def interleaved(dst):
+    return dst.rearrange("p (c i t) -> p c t i", i=4, t=PACK)
+
+
+def planes(src):
+    return src.rearrange("p t (c i) -> p c t i", i=4)
+
+
+def scale_rows_in(queue, tile, rows):
+    for q in range(4):
+        queue.dma_start(out=tile[32 * q : 32 * q + 4, :].bitcast(I32), in_=rows[4 * q : 4 * q + 4, :].bitcast(I32))
+
+
+def tile_picked_sendres_none_po_kernel(
+    tc, x_words, x_scales, w1, w2, w3_words, w3_scales, res, offs, n1, n2, dst, out_0, out_1, out_2
+):
+    nc = tc.nc
+    with ExitStack() as ctx:
+        lists = ctx.enter_context(tc.tile_pool(name="lists", bufs=1))
+        sb = ctx.enter_context(tc.tile_pool(name="sb", bufs=1))
+        psum = ctx.enter_context(tc.psum_pool(name="psum", bufs=8))
+
+        offs_sb = lists.tile([P, S // 16], U16, name="offs_sb")
+        n1_sb = lists.tile([P, S // 16], U16, name="n1_sb")
+        n2_sb = lists.tile([P, S // 16], U16, name="n2_sb")
+        dst_sb = lists.tile([P, S // 16], U16, name="dst_sb")
+
+        xs_table = sb.tile([P, T], U8, name="xs_table", align_bytes=64)
+        w3s_raw = sb.tile([P, N], U8, name="w3s_raw", align_bytes=64)
+        nc.vector.memset(xs_table[:].bitcast(I32), 0)
+        nc.gpsimd.memset(w3s_raw[:].bitcast(I32), 0)
+
+        nc.sync.dma_start(offs_sb[:], offs)
+        w1_raw = [sb.tile([P, PACK, HALF], F32, name="w1_raw%d" % a) for a in range(2)]
+        w1_view = w1.rearrange("(p j) c -> p j c", j=PACK)
+        for a in range(2):
+            nc.sync.dma_start(out=w1_raw[a][:], in_=w1_view[:, :, a * HALF : (a + 1) * HALF])
+        scale_rows_in(nc.scalar, xs_table, x_scales[0])
+        xw_table = sb.tile([P, T], U32, name="xw_table", align_bytes=64)
+        nc.sync.dma_start(out=xw_table[:].bitcast(I32), in_=x_words[0].rearrange("p n t -> p (n t)").bitcast(I32))
+        w3w_raw = sb.tile([P, N], U32, name="w3w_raw", align_bytes=64)
+        nc.sync.dma_start(out=w3w_raw[:].bitcast(I32), in_=w3_words[0].rearrange("p n t -> p (n t)").bitcast(I32))
+        nc.sync.dma_start(n1_sb[:], n1)
+        nc.sync.dma_start(n2_sb[:], n2)
+        w2_raw = sb.tile([P, PACK, H], F32, name="w2_raw")
+        nc.sync.dma_start(out=w2_raw[:], in_=w2.rearrange("(p j) c -> p j c", j=PACK))
+        nc.sync.dma_start(dst_sb[:], dst)
+        scale_rows_in(nc.sync, w3s_raw, w3_scales[0])
+        res_sb = sb.tile([P, PACK, S], F32, name="res_sb")
+        nc.sync.dma_start(out=res_sb[:], in_=res.rearrange("(p t) c -> p t c", t=PACK))
+
+        xs = sb.tile([P, S], U8, name="xs", align_bytes=64)
+        nc.vector.tensor_copy(out=xs[:], in_=xs_table[:].indirect(offs_sb[:]))
+        w1_bf = sb.tile([P, PACK * H], BF16, name="w1_bf", align_bytes=64)
+        w1_dealt = w1_bf[:].rearrange("p (t m j) -> p m j t", t=PACK, j=PACK)
+        for a in range(2):
+            src = w1_raw[a][:].rearrange("p j (m t) -> p m j t", t=PACK)
+            m0 = a * 64
+            nc.vector.tensor_copy(out=w1_dealt[:, m0 : m0 + W_VEC], in_=src[:, 0:W_VEC])
+            nc.scalar.activation(out=w1_dealt[:, m0 + W_VEC : m0 + 64], in_=src[:, W_VEC:64], func=ACT.Copy)
+        w1_q = sb.tile([P, H], U32, name="w1_q", align_bytes=64)
+        w1_s = sb.tile([P, H], U8, name="w1_s", align_bytes=64)
+        nc.vector.quantize_mx(out=w1_q[:].bitcast(FP8X4), scales=w1_s[:], in_=w1_bf[:])
+
+        xw = [sb.tile([P, HALF], U32, name="xw%d" % a, align_bytes=64) for a in range(2)]
+        for a in range(2):
+            nc.vector.tensor_copy(out=xw[a][:], in_=xw_table[:].indirect(offs_sb[:, a * LIST_COLS : (a + 1) * LIST_COLS]))
+
+        y_neg = [sb.tile([P, S], F32, name="y_neg%d" % t) for t in range(PACK)]
+        y_sb = sb.tile([P, PACK, S], F32, name="y_sb")
+        y_ps = {}
+        for t in range(PACK):
+            cols = slice(t * P, (t + 1) * P)
+            for a in range(2):
+                bank = psum.tile([P, S], F32, name="bank", tag="bank")
+                nc.tensor.matmul_mx(
+                    out=bank[:, 0:HALF], lhsT=w1_q[:, cols].bitcast(FP8X4), lhsT_scale=w1_s[:, cols],
+                    rhs=xw[a][:].bitcast(FP8X4), rhs_scale=xs[:, a * HALF : (a + 1) * HALF], start=True, stop=True,
+                )
+                y_ps[(t, a)] = bank
+            for a in range(2):
+                nc.scalar.activation(out=y_neg[t][:, a * HALF : (a + 1) * HALF], in_=y_ps[(t, a)][:, 0:HALF], func=ACT.Copy, scale=-1.0)
+            nc.scalar.copy(out=y_sb[:, t, 0:HALF], in_=y_ps[(t, 0)][:, 0:HALF])
+        for t in range(PACK):
+            nc.scalar.copy(out=y_sb[:, t, HALF:S], in_=y_ps[(t, 1)][:, 0:HALF])
+
+        w3_q = sb.tile([P, N], U32, name="w3_q", align_bytes=64)
+        w3_s = sb.tile([P, N], U8, name="w3_s", align_bytes=64)
+        nc.vector.tensor_copy(out=w3_q[:].rearrange("p (t m) -> p m t", t=PACK), in_=w3w_raw[:].rearrange("p (m t) -> p m t", t=PACK))
+        nc.vector.tensor_copy(out=w3_s[:].rearrange("p (t m) -> p m t", t=PACK), in_=w3s_raw[:].rearrange("p (m t) -> p m t", t=PACK))
+
+        w2_bf = sb.tile([P, PACK * H], BF16, name="w2_bf", align_bytes=64)
+        nc.scalar.activation(
+            out=w2_bf[:].rearrange("p (t m j) -> p m j t", t=PACK, j=PACK),
+            in_=w2_raw[:].rearrange("p j (m t) -> p m j t", t=PACK), func=ACT.Copy,
+        )
+        w2_q = sb.tile([P, H], U32, name="w2_q", align_bytes=64)
+        w2_s = sb.tile([P, H], U8, name="w2_s", align_bytes=64)
+
+        hr = []
+        for a in range(2):
+            half = slice(a * HALF, (a + 1) * HALF)
+            entries = slice(a * LIST_COLS, (a + 1) * LIST_COLS)
+            d1 = sb.tile([P, PACK, HALF], F32, name="d1_%d" % a)
+            d2 = sb.tile([P, PACK, HALF], F32, name="d2_%d" % a)
+            for t in range(PACK):
+                nc.vector.tensor_tensor(out=d1[:, t, :], in0=y_neg[t][:].indirect(n1_sb[:, entries]), in1=y_sb[:, t, half], op=ALU.add)
+                nc.vector.tensor_tensor(out=d2[:, t, :], in0=y_neg[t][:].indirect(n2_sb[:, entries]), in1=y_sb[:, t, half], op=ALU.add)
+            z_bf = sb.tile([P, PACK * HALF], BF16, name="z_bf%d" % a, align_bytes=64)
+            nc.vector.tensor_tensor(out=interleaved(z_bf[:]), in0=planes(d1[:]), in1=planes(d2[:]), op=ALU.min)
+            if a == 0:
+                nc.vector.quantize_mx(out=w2_q[:].bitcast(FP8X4), scales=w2_s[:], in_=w2_bf[:])
+            z_q = sb.tile([P, HALF], U32, name="z_q%d" % a, align_bytes=64)
+            z_s = sb.tile([P, HALF], U8, name="z_s%d" % a, align_bytes=64)
+            nc.vector.quantize_mx(out=z_q[:].bitcast(FP8X4), scales=z_s[:], in_=z_bf[:])
+            hr_a = sb.tile([P, PACK, HALF], F32, name="hr%d" % a)
+            for u in range(2):
+                bank = psum.tile([P, S], F32, name="bank", tag="bank")
+                for e in range(2):
+                    cols = slice((2 * u + e) * P, (2 * u + e + 1) * P)
+                    nc.tensor.matmul_mx(
+                        out=bank[:, e * HALF : (e + 1) * HALF], lhsT=w2_q[:, cols].bitcast(FP8X4), lhsT_scale=w2_s[:, cols],
+                        rhs=z_q[:].bitcast(FP8X4), rhs_scale=z_s[:], start=True, stop=True,
+                    )
+                nc.scalar.activation(out=hr_a[:, 2 * u : 2 * u + 2, :].rearrange("p e c -> p (e c)"), in_=bank[:], func=ACT.Relu)
+            hr.append(hr_a)
+
+        hs = [sb.tile([P, S], F32, name="hs%d" % t) for t in range(PACK)]
+        hs_all = sb.tile([P, PACK, S], F32, name="hs_all")
+        for a in range(2):
+            entries = slice(a * LIST_COLS, (a + 1) * LIST_COLS)
+            for t in range(PACK):
+                nc.vector.tensor_copy(out=hs[t][:].indirect(dst_sb[:, entries]), in_=hr[a][:, t, :])
+        for t in range(PACK - 1):
+            nc.scalar.copy(out=hs_all[:, t, :], in_=hs[t][:])
+        for b in range(S // BLOCK):
+            cols = slice(b * BLOCK, (b + 1) * BLOCK)
+            nc.scalar.copy(out=hs_all[:, PACK - 1, cols], in_=hs[PACK - 1][:, cols])
+
+        out_view = out_0.rearrange("(p t) c -> p t c", t=PACK)
+        words_view = out_1[0].rearrange("p n t -> p (n t)").bitcast(I32)
+        o_q = sb.tile([P, S], U32, name="o_q", align_bytes=64)
+        o_s = sb.tile([P, S], U8, name="o_s", align_bytes=64)
+        nblocks = S // BLOCK
+        z2_bf, banks, o_f, o_bf = {}, {}, {}, {}
+
+        def subtract(b):
+            cols = slice(b * BLOCK, (b + 1) * BLOCK)
+            z2_bf[b] = sb.tile([P, PACK * BLOCK], BF16, name="z2_bf%d" % b, align_bytes=64)
+            nc.vector.tensor_tensor(out=interleaved(z2_bf[b][:]), in0=planes(hs_all[:, :, cols]), in1=planes(y_sb[:, :, cols]), op=ALU.subtract)
+
+        def multiply(b):
+            z2_q = sb.tile([P, BLOCK], U32, name="z2_q%d" % b, align_bytes=64)
+            z2_s = sb.tile([P, BLOCK], U8, name="z2_s%d" % b, align_bytes=64)
+            nc.vector.quantize_mx(out=z2_q[:].bitcast(FP8X4), scales=z2_s[:], in_=z2_bf[b][:])
+            banks[b] = psum.tile([P, S], F32, name="bank", tag="bank")
+            for t in range(PACK):
+                cols = slice(t * P, (t + 1) * P)
+                nc.tensor.matmul_mx(
+                    out=banks[b][:, t * BLOCK : (t + 1) * BLOCK], lhsT=w3_q[:, cols].bitcast(FP8X4), lhsT_scale=w3_s[:, cols],
+                    rhs=z2_q[:].bitcast(FP8X4), rhs_scale=z2_s[:], start=True, stop=True,
+                )
+
+        def add_residual(b):
+            cols = slice(b * BLOCK, (b + 1) * BLOCK)
+            o_f[b] = sb.tile([P, PACK, BLOCK], F32, name="o_f%d" % b)
+            nc.vector.tensor_tensor(out=o_f[b][:], in0=banks[b][:].rearrange("p (t c) -> p t c", t=PACK), in1=res_sb[:, :, cols], op=ALU.add)
+            nc.sync.dma_start(out=out_view[:, :, cols], in_=o_f[b][:])
+            o_bf[b] = sb.tile([P, PACK * BLOCK], BF16, name="o_bf%d" % b, align_bytes=64)
+            nc.scalar.copy(out=interleaved(o_bf[b][:]), in_=planes(o_f[b][:]))
+
+        def hand_on(b):
+            cols = slice(b * BLOCK, (b + 1) * BLOCK)
+            nc.vector.quantize_mx(out=o_q[:, cols].bitcast(FP8X4), scales=o_s[:, cols], in_=o_bf[b][:])
+            nc.sync.dma_start(out=words_view[:, cols], in_=o_q[:, cols].bitcast(I32))
+
+        for step in range(nblocks + 3):
+            if step < nblocks:
+                subtract(step)
+            if 0 <= step - 2 < nblocks:
+                add_residual(step - 2)
+            if 0 <= step - 1 < nblocks:
+                multiply(step - 1)
+            if 0 <= step - 3 < nblocks:
+                hand_on(step - 3)
+        for q in range(4):
+            queue = nc.scalar if q % 2 else nc.sync
+            queue.dma_start(out=out_2[0][4 * q : 4 * q + 4, :].bitcast(I32), in_=o_s[32 * q : 32 * q + 4, :].bitcast(I32))

@@ -1,6 +1,7 @@
 from contextlib import ExitStack
 
 import concourse.mybir as mybir
+from concourse.masks import make_identity
 
 K, T, S, N, H = 512, 2048, 512, 512, 512
 FLOPS = 2 * S * (K * H + H * H + H * N)
@@ -20,6 +21,7 @@ PACK = 4
 HALF = S // 2
 LIST_COLS = HALF // 16
 BLOCK = 128
+RAW = PACK * HALF * 4
 W_VEC = 40
 
 
@@ -43,6 +45,11 @@ def tile_picked_sendres_none_po_kernel(
     with ExitStack() as ctx:
         lists = ctx.enter_context(tc.tile_pool(name="lists", bufs=1))
         sb = ctx.enter_context(tc.tile_pool(name="sb", bufs=1))
+        shared = ctx.enter_context(tc.tile_pool(name="shared", bufs=1))
+        stage = ctx.enter_context(tc.tile_pool(name="stage", bufs=1))
+        late = ctx.enter_context(tc.tile_pool(name="late", bufs=1))
+        held = ctx.enter_context(tc.tile_pool(name="held", bufs=1))
+        early = ctx.enter_context(tc.tile_pool(name="early", bufs=1))
         psum = ctx.enter_context(tc.psum_pool(name="psum", bufs=8))
 
         offs_sb = lists.tile([P, S // 16], U16, name="offs_sb")
@@ -55,24 +62,21 @@ def tile_picked_sendres_none_po_kernel(
         nc.vector.memset(xs_table[:].bitcast(I32), 0)
         nc.gpsimd.memset(w3s_raw[:].bitcast(I32), 0)
 
+
         nc.sync.dma_start(offs_sb[:], offs)
-        w1_raw = [sb.tile([P, PACK, HALF], F32, name="w1_raw%d" % a) for a in range(2)]
+        nc.sync.dma_start(n1_sb[:], n1)
+        nc.sync.dma_start(n2_sb[:], n2)
+        w1_raw = [stage.tile([P, PACK, HALF], F32, name="w1_raw%d" % a, offset=a * RAW) for a in range(2)]
         w1_view = w1.rearrange("(p j) c -> p j c", j=PACK)
         for a in range(2):
             nc.sync.dma_start(out=w1_raw[a][:], in_=w1_view[:, :, a * HALF : (a + 1) * HALF])
         scale_rows_in(nc.scalar, xs_table, x_scales[0])
-        xw_table = sb.tile([P, T], U32, name="xw_table", align_bytes=64)
+        scale_rows_in(nc.gpsimd, w3s_raw, w3_scales[0])
+        ident = sb.tile([P, P], F32, name="ident")
+        make_identity(nc, ident[:])
+        xw_table = shared.tile([P, T], U32, name="xw_table", align_bytes=64, offset=0)
         nc.sync.dma_start(out=xw_table[:].bitcast(I32), in_=x_words[0].rearrange("p n t -> p (n t)").bitcast(I32))
-        w3w_raw = sb.tile([P, N], U32, name="w3w_raw", align_bytes=64)
-        nc.sync.dma_start(out=w3w_raw[:].bitcast(I32), in_=w3_words[0].rearrange("p n t -> p (n t)").bitcast(I32))
-        nc.sync.dma_start(n1_sb[:], n1)
-        nc.sync.dma_start(n2_sb[:], n2)
-        w2_raw = sb.tile([P, PACK, H], F32, name="w2_raw")
-        nc.sync.dma_start(out=w2_raw[:], in_=w2.rearrange("(p j) c -> p j c", j=PACK))
         nc.sync.dma_start(dst_sb[:], dst)
-        scale_rows_in(nc.sync, w3s_raw, w3_scales[0])
-        res_sb = sb.tile([P, PACK, S], F32, name="res_sb")
-        nc.sync.dma_start(out=res_sb[:], in_=res.rearrange("(p t) c -> p t c", t=PACK))
 
         xs = sb.tile([P, S], U8, name="xs", align_bytes=64)
         nc.vector.tensor_copy(out=xs[:], in_=xs_table[:].indirect(offs_sb[:]))
@@ -83,96 +87,184 @@ def tile_picked_sendres_none_po_kernel(
             m0 = a * 64
             nc.vector.tensor_copy(out=w1_dealt[:, m0 : m0 + W_VEC], in_=src[:, 0:W_VEC])
             nc.scalar.activation(out=w1_dealt[:, m0 + W_VEC : m0 + 64], in_=src[:, W_VEC:64], func=ACT.Copy)
+        w3w_raw = stage.tile([P, N], U32, name="w3w_raw", offset=0)
+        nc.sync.dma_start(out=w3w_raw[:].bitcast(I32), in_=w3_words[0].rearrange("p n t -> p (n t)").bitcast(I32))
+        w2_raw = stage.tile([P, PACK, H], F32, name="w2_raw", offset=RAW)
+        nc.sync.dma_start(out=w2_raw[:], in_=w2.rearrange("(p j) c -> p j c", j=PACK))
         w1_q = sb.tile([P, H], U32, name="w1_q", align_bytes=64)
         w1_s = sb.tile([P, H], U8, name="w1_s", align_bytes=64)
         nc.vector.quantize_mx(out=w1_q[:].bitcast(FP8X4), scales=w1_s[:], in_=w1_bf[:])
 
-        xw = [sb.tile([P, HALF], U32, name="xw%d" % a, align_bytes=64) for a in range(2)]
+        xw = [late.tile([P, HALF], U32, name="xw%d" % a, align_bytes=64, offset=a * 4 * HALF) for a in range(2)]
         for a in range(2):
             nc.vector.tensor_copy(out=xw[a][:], in_=xw_table[:].indirect(offs_sb[:, a * LIST_COLS : (a + 1) * LIST_COLS]))
 
-        y_neg = [sb.tile([P, S], F32, name="y_neg%d" % t) for t in range(PACK)]
-        y_sb = sb.tile([P, PACK, S], F32, name="y_sb")
-        y_ps = {}
-        for t in range(PACK):
-            cols = slice(t * P, (t + 1) * P)
-            for a in range(2):
-                bank = psum.tile([P, S], F32, name="bank", tag="bank")
-                nc.tensor.matmul_mx(
-                    out=bank[:, 0:HALF], lhsT=w1_q[:, cols].bitcast(FP8X4), lhsT_scale=w1_s[:, cols],
-                    rhs=xw[a][:].bitcast(FP8X4), rhs_scale=xs[:, a * HALF : (a + 1) * HALF], start=True, stop=True,
-                )
-                y_ps[(t, a)] = bank
-            for a in range(2):
-                nc.scalar.activation(out=y_neg[t][:, a * HALF : (a + 1) * HALF], in_=y_ps[(t, a)][:, 0:HALF], func=ACT.Copy, scale=-1.0)
-            nc.scalar.copy(out=y_sb[:, t, 0:HALF], in_=y_ps[(t, 0)][:, 0:HALF])
-        for t in range(PACK):
-            nc.scalar.copy(out=y_sb[:, t, HALF:S], in_=y_ps[(t, 1)][:, 0:HALF])
+        y_win = [sb.tile([P, S], F32, name="y_win%d" % t) for t in range(PACK)]
+        y_neg = sb.tile([P, PACK, S], F32, name="y_neg")
 
-        w3_q = sb.tile([P, N], U32, name="w3_q", align_bytes=64)
-        w3_s = sb.tile([P, N], U8, name="w3_s", align_bytes=64)
+        def first_layer(t, a):
+            cols = slice(t * P, (t + 1) * P)
+            half = slice(a * HALF, (a + 1) * HALF)
+            bank = psum.tile([P, S], F32, name="bank", tag="bank")
+            nc.tensor.matmul_mx(
+                out=bank[:, 0:HALF], lhsT=w1_q[:, cols].bitcast(FP8X4), lhsT_scale=w1_s[:, cols],
+                rhs=xw[a][:].bitcast(FP8X4), rhs_scale=xs[:, half], start=True, stop=True,
+            )
+            nc.scalar.copy(out=y_win[t][:, half], in_=bank[:, 0:HALF])
+            if a == 0:
+                nc.scalar.activation(out=y_neg[:, t, half], in_=bank[:, 0:HALF], func=ACT.Copy, scale=-1.0)
+
+        for t in range(PACK):
+            for a in range(2):
+                first_layer(t, a)
+
+        w3_q = shared.tile([P, N], U32, name="w3_q", align_bytes=64, offset=0)
+        w3_s = shared.tile([P, N], U8, name="w3_s", align_bytes=64, offset=4 * N)
         nc.vector.tensor_copy(out=w3_q[:].rearrange("p (t m) -> p m t", t=PACK), in_=w3w_raw[:].rearrange("p (m t) -> p m t", t=PACK))
         nc.vector.tensor_copy(out=w3_s[:].rearrange("p (t m) -> p m t", t=PACK), in_=w3s_raw[:].rearrange("p (m t) -> p m t", t=PACK))
 
-        w2_bf = sb.tile([P, PACK * H], BF16, name="w2_bf", align_bytes=64)
-        nc.scalar.activation(
-            out=w2_bf[:].rearrange("p (t m j) -> p m j t", t=PACK, j=PACK),
-            in_=w2_raw[:].rearrange("p j (m t) -> p m j t", t=PACK), func=ACT.Copy,
-        )
+        w2_bf = late.tile([P, PACK * H], BF16, name="w2_bf", align_bytes=64, offset=0)
+        w2_dealt = w2_bf[:].rearrange("p (t m j) -> p m j t", t=PACK, j=PACK)
+        w2_src = w2_raw[:].rearrange("p j (m t) -> p m j t", t=PACK)
         w2_q = sb.tile([P, H], U32, name="w2_q", align_bytes=64)
         w2_s = sb.tile([P, H], U8, name="w2_s", align_bytes=64)
 
-        hr = []
-        for a in range(2):
-            half = slice(a * HALF, (a + 1) * HALF)
-            entries = slice(a * LIST_COLS, (a + 1) * LIST_COLS)
-            d1 = sb.tile([P, PACK, HALF], F32, name="d1_%d" % a)
-            d2 = sb.tile([P, PACK, HALF], F32, name="d2_%d" % a)
-            for t in range(PACK):
-                nc.vector.tensor_tensor(out=d1[:, t, :], in0=y_neg[t][:].indirect(n1_sb[:, entries]), in1=y_sb[:, t, half], op=ALU.add)
-                nc.vector.tensor_tensor(out=d2[:, t, :], in0=y_neg[t][:].indirect(n2_sb[:, entries]), in1=y_sb[:, t, half], op=ALU.add)
-            z_bf = sb.tile([P, PACK * HALF], BF16, name="z_bf%d" % a, align_bytes=64)
-            nc.vector.tensor_tensor(out=interleaved(z_bf[:]), in0=planes(d1[:]), in1=planes(d2[:]), op=ALU.min)
-            if a == 0:
-                nc.vector.quantize_mx(out=w2_q[:].bitcast(FP8X4), scales=w2_s[:], in_=w2_bf[:])
-            z_q = sb.tile([P, HALF], U32, name="z_q%d" % a, align_bytes=64)
-            z_s = sb.tile([P, HALF], U8, name="z_s%d" % a, align_bytes=64)
-            nc.vector.quantize_mx(out=z_q[:].bitcast(FP8X4), scales=z_s[:], in_=z_bf[:])
-            hr_a = sb.tile([P, PACK, HALF], F32, name="hr%d" % a)
-            for u in range(2):
-                bank = psum.tile([P, S], F32, name="bank", tag="bank")
-                for e in range(2):
-                    cols = slice((2 * u + e) * P, (2 * u + e + 1) * P)
-                    nc.tensor.matmul_mx(
-                        out=bank[:, e * HALF : (e + 1) * HALF], lhsT=w2_q[:, cols].bitcast(FP8X4), lhsT_scale=w2_s[:, cols],
-                        rhs=z_q[:].bitcast(FP8X4), rhs_scale=z_s[:], start=True, stop=True,
-                    )
-                nc.scalar.activation(out=hr_a[:, 2 * u : 2 * u + 2, :].rearrange("p e c -> p (e c)"), in_=bank[:], func=ACT.Relu)
-            hr.append(hr_a)
+        second, gap, lift, sums, turned, z_bf, h_ps = {}, {}, {}, {}, {}, {}, {}
+        hr = sb.tile([P, PACK, S], F32, name="hr")
 
-        hs = [sb.tile([P, S], F32, name="hs%d" % t) for t in range(PACK)]
-        hs_all = sb.tile([P, PACK, S], F32, name="hs_all")
-        for a in range(2):
-            entries = slice(a * LIST_COLS, (a + 1) * LIST_COLS)
+        def negate(a):
             for t in range(PACK):
-                nc.vector.tensor_copy(out=hs[t][:].indirect(dst_sb[:, entries]), in_=hr[a][:, t, :])
+                half = slice(a * HALF, (a + 1) * HALF)
+                nc.scalar.activation(out=y_neg[:, t, half], in_=y_win[t][:, half], func=ACT.Copy, scale=-1.0)
+
+        def fetch_second(unit):
+            a, t = divmod(unit, PACK)
+            if unit >= 6:
+                second[unit] = early.tile([P, HALF], F32, name="second%d" % unit, align_bytes=64, offset=(unit - 6) * 4 * HALF)
+            else:
+                second[unit] = sb.tile([P, HALF], F32, name="second%d" % unit)
+            nc.vector.tensor_copy(out=second[unit][:], in_=y_win[t][:].indirect(n2_sb[:, a * LIST_COLS : (a + 1) * LIST_COLS]))
+
+        def fetch_gap(unit):
+            a, t = divmod(unit, PACK)
+            gap[unit] = sb.tile([P, HALF], F32, name="gap%d" % unit)
+            nc.vector.tensor_tensor(
+                out=gap[unit][:], in0=y_win[t][:].indirect(n1_sb[:, a * LIST_COLS : (a + 1) * LIST_COLS]), in1=second[unit][:], op=ALU.subtract
+            )
+
+        def add_up(unit):
+            a, t = divmod(unit, PACK)
+            lift[unit] = sb.tile([P, HALF], F32, name="lift%d" % unit)
+            nc.scalar.activation(out=lift[unit][:], in_=gap[unit][:], func=ACT.Relu)
+            for i in range(2):
+                b = 2 * a + i
+                if t == 0:
+                    sums[b] = psum.tile([P, S], F32, name="bank", tag="bank")
+                part = slice(i * BLOCK, (i + 1) * BLOCK)
+                terms = (y_neg[:, t, b * BLOCK : (b + 1) * BLOCK], second[unit][:, part], lift[unit][:, part])
+                for n, term in enumerate(terms):
+                    nc.tensor.matmul(sums[b][:, t * P : (t + 1) * P], lhsT=term, rhs=ident[:], is_transpose=True, start=(n == 0), stop=(n == 2))
+
+        def turn_back(b):
+            pairs = sb.tile([P, PACK * P], BF16, name="pairs%d" % b)
+            nc.scalar.activation(
+                out=pairs[:].rearrange("c (u p e) -> c u p e", u=2, e=2), in_=sums[b][:].rearrange("c (u e p) -> c u p e", u=2, e=2),
+                func=ACT.Copy,
+            )
+            turned[b] = psum.tile([P, S], F32, name="bank", tag="bank")
+            for u in range(2):
+                nc.tensor.transpose(turned[b][:, u * BLOCK : (u + 1) * BLOCK], pairs[:].bitcast(F32)[:, u * P : (u + 1) * P], ident[:])
+
+        def weave(b, tile, at):
+            nc.scalar.copy(
+                out=tile[:].bitcast(F32)[:, at * 2 * BLOCK : (at + 1) * 2 * BLOCK].rearrange("p (c u) -> p c u", u=2),
+                in_=turned[b][:, 0 : 2 * BLOCK].rearrange("p (u c) -> p c u", u=2),
+            )
+
+        def second_layer(name, tile, width):
+            z_q = sb.tile([P, width], U32, name="z_q%d" % name, align_bytes=64)
+            z_s = sb.tile([P, width], U8, name="z_s%d" % name, align_bytes=64)
+            nc.vector.quantize_mx(out=z_q[:].bitcast(FP8X4), scales=z_s[:], in_=tile[:])
+            per_bank = S // width
+            for t in range(PACK):
+                if t % per_bank == 0:
+                    bank = psum.tile([P, S], F32, name="bank", tag="bank")
+                at = slice((t % per_bank) * width, (t % per_bank + 1) * width)
+                cols = slice(t * P, (t + 1) * P)
+                nc.tensor.matmul_mx(
+                    out=bank[:, at], lhsT=w2_q[:, cols].bitcast(FP8X4), lhsT_scale=w2_s[:, cols],
+                    rhs=z_q[:].bitcast(FP8X4), rhs_scale=z_s[:], start=True, stop=True,
+                )
+                h_ps[(name, t)] = (bank, t % per_bank)
+
+        def relu_out(name, t0, count, c0, width):
+            bank, at = h_ps[(name, t0)]
+            nc.scalar.activation(
+                out=hr[:, t0 : t0 + count, c0 : c0 + width],
+                in_=bank[:, at * width : (at + count) * width].rearrange("p (t c) -> p t c", t=count), func=ACT.Relu, scale=-1.0,
+            )
+
+        hs = [sb.tile([P, S], F32, name="hs%d" % t) for t in range(PACK - 1)]
+        z_bf[0] = early.tile([P, PACK * HALF], BF16, name="z_bf0", align_bytes=64, offset=0)
+        z_bf[1] = held.tile([P, PACK * HALF], BF16, name="z_bf1", align_bytes=64, offset=0)
+
+        def send(t, c0, width):
+            nc.vector.tensor_copy(out=hs[t][:].indirect(dst_sb[:, c0 // 16 : (c0 + width) // 16]), in_=hr[:, t, c0 : c0 + width])
+
+        d1 = sb.tile([P, PACK, HALF], F32, name="d1")
+        d2 = sb.tile([P, PACK, HALF], F32, name="d2")
+        for t in range(PACK):
+            nc.vector.tensor_tensor(out=d1[:, t, :], in0=y_win[t][:].indirect(n1_sb[:, 0:LIST_COLS]), in1=y_neg[:, t, 0:HALF], op=ALU.add)
+            nc.vector.tensor_tensor(out=d2[:, t, :], in0=y_win[t][:].indirect(n2_sb[:, 0:LIST_COLS]), in1=y_neg[:, t, 0:HALF], op=ALU.add)
+        nc.scalar.activation(out=w2_dealt, in_=w2_src, func=ACT.Copy)
+        negate(1)
+        fetch_second(4)
+        nc.vector.tensor_tensor(out=interleaved(z_bf[0][:]), in0=planes(d1[:]), in1=planes(d2[:]), op=ALU.max)
+        fetch_second(5)
+        nc.vector.quantize_mx(out=w2_q[:].bitcast(FP8X4), scales=w2_s[:], in_=w2_bf[:])
+        second_layer(0, z_bf[0], HALF)
+        for unit in range(PACK, 2 * PACK):
+            if unit + 2 < 2 * PACK:
+                fetch_second(unit + 2)
+            fetch_gap(unit)
+            add_up(unit)
+            if unit % 2 == 0:
+                relu_out(0, unit - PACK, 2, 0, HALF)
+        turn_back(2)
+        turn_back(3)
+        weave(2, z_bf[1], 0)
+        weave(3, z_bf[1], 1)
+        for t in range(PACK - 1):
+            send(t, 0, HALF)
+        second_layer(1, z_bf[1], HALF)
+        hs.append(held.tile([P, S], F32, name="hs3", align_bytes=64, offset=0))
+        send(PACK - 1, 0, HALF)
+        relu_out(1, 0, 2, HALF, HALF)
+        relu_out(1, 2, 2, HALF, HALF)
+        for t in range(PACK):
+            send(t, HALF, HALF)
+
+        hs_all = sb.tile([P, PACK, S], F32, name="hs_all")
         for t in range(PACK - 1):
             nc.scalar.copy(out=hs_all[:, t, :], in_=hs[t][:])
         for b in range(S // BLOCK):
             cols = slice(b * BLOCK, (b + 1) * BLOCK)
             nc.scalar.copy(out=hs_all[:, PACK - 1, cols], in_=hs[PACK - 1][:, cols])
 
+        res_sb = stage.tile([P, PACK, S], F32, name="res_sb", offset=RAW)
+        nc.sync.dma_start(out=res_sb[:], in_=res.rearrange("(p t) c -> p t c", t=PACK))
         out_view = out_0.rearrange("(p t) c -> p t c", t=PACK)
         words_view = out_1[0].rearrange("p n t -> p (n t)").bitcast(I32)
         o_q = sb.tile([P, S], U32, name="o_q", align_bytes=64)
         o_s = sb.tile([P, S], U8, name="o_s", align_bytes=64)
         nblocks = S // BLOCK
-        z2_bf, banks, o_f, o_bf = {}, {}, {}, {}
+        z2_bf, banks, o_f = {}, {}, {}
+        o_bf = sb.tile([P, PACK * S], BF16, name="o_bf", align_bytes=64)
 
         def subtract(b):
             cols = slice(b * BLOCK, (b + 1) * BLOCK)
             z2_bf[b] = sb.tile([P, PACK * BLOCK], BF16, name="z2_bf%d" % b, align_bytes=64)
-            nc.vector.tensor_tensor(out=interleaved(z2_bf[b][:]), in0=planes(hs_all[:, :, cols]), in1=planes(y_sb[:, :, cols]), op=ALU.subtract)
+            nc.vector.tensor_tensor(out=interleaved(z2_bf[b][:]), in0=planes(hs_all[:, :, cols]), in1=planes(y_neg[:, :, cols]), op=ALU.add)
 
         def multiply(b):
             z2_q = sb.tile([P, BLOCK], U32, name="z2_q%d" % b, align_bytes=64)
@@ -191,23 +283,24 @@ def tile_picked_sendres_none_po_kernel(
             o_f[b] = sb.tile([P, PACK, BLOCK], F32, name="o_f%d" % b)
             nc.vector.tensor_tensor(out=o_f[b][:], in0=banks[b][:].rearrange("p (t c) -> p t c", t=PACK), in1=res_sb[:, :, cols], op=ALU.add)
             nc.sync.dma_start(out=out_view[:, :, cols], in_=o_f[b][:])
-            o_bf[b] = sb.tile([P, PACK * BLOCK], BF16, name="o_bf%d" % b, align_bytes=64)
-            nc.scalar.copy(out=interleaved(o_bf[b][:]), in_=planes(o_f[b][:]))
+            nc.scalar.copy(out=interleaved(o_bf[:, PACK * b * BLOCK : PACK * (b + 1) * BLOCK]), in_=planes(o_f[b][:]))
 
-        def hand_on(b):
-            cols = slice(b * BLOCK, (b + 1) * BLOCK)
-            nc.vector.quantize_mx(out=o_q[:, cols].bitcast(FP8X4), scales=o_s[:, cols], in_=o_bf[b][:])
+        def hand_on(b0, b1):
+            cols = slice(b0 * BLOCK, b1 * BLOCK)
+            nc.vector.quantize_mx(out=o_q[:, cols].bitcast(FP8X4), scales=o_s[:, cols], in_=o_bf[:, PACK * b0 * BLOCK : PACK * b1 * BLOCK])
             nc.sync.dma_start(out=words_view[:, cols], in_=o_q[:, cols].bitcast(I32))
 
-        for step in range(nblocks + 3):
-            if step < nblocks:
-                subtract(step)
-            if 0 <= step - 2 < nblocks:
-                add_residual(step - 2)
-            if 0 <= step - 1 < nblocks:
-                multiply(step - 1)
-            if 0 <= step - 3 < nblocks:
-                hand_on(step - 3)
+        for b in range(nblocks):
+            subtract(b)
+            if b >= 1:
+                multiply(b - 1)
+        add_residual(0)
+        multiply(nblocks - 1)
+        for b in range(1, nblocks):
+            add_residual(b)
+        hand_on(0, 2)
+        hand_on(2, 3)
+        hand_on(3, 4)
         for q in range(4):
-            queue = nc.scalar if q % 2 else nc.sync
+            queue = nc.sync if q == 0 else nc.scalar
             queue.dma_start(out=out_2[0][4 * q : 4 * q + 4, :].bitcast(I32), in_=o_s[32 * q : 32 * q + 4, :].bitcast(I32))

from contextlib import ExitStack

import concourse.mybir as mybir
from concourse.masks import make_identity

K, T, S, N, H = 512, 2048, 512, 512, 512
FLOPS = 2 * S * (K * H + H * H + H * N)

F32 = mybir.dt.float32
BF16 = mybir.dt.bfloat16
I32 = mybir.dt.int32
U32 = mybir.dt.uint32
U16 = mybir.dt.uint16
U8 = mybir.dt.uint8
FP8X4 = mybir.dt.float8_e4m3fn_x4
ALU = mybir.AluOpType
ACT = mybir.ActivationFunctionType

P = 128
PACK = 4
HALF = S // 2
LIST_COLS = HALF // 16
BLOCK = 128
RAW = PACK * HALF * 4
W_VEC = 40


def interleaved(dst):
    return dst.rearrange("p (c i t) -> p c t i", i=4, t=PACK)


def planes(src):
    return src.rearrange("p t (c i) -> p c t i", i=4)


def scale_rows_in(queue, tile, rows):
    for q in range(4):
        queue.dma_start(out=tile[32 * q : 32 * q + 4, :].bitcast(I32), in_=rows[4 * q : 4 * q + 4, :].bitcast(I32))


def tile_picked_sendres_none_po_kernel(
    tc, x_words, x_scales, w1, w2, w3_words, w3_scales, res, offs, n1, n2, dst, out_0, out_1, out_2
):
    nc = tc.nc
    with ExitStack() as ctx:
        lists = ctx.enter_context(tc.tile_pool(name="lists", bufs=1))
        sb = ctx.enter_context(tc.tile_pool(name="sb", bufs=1))
        shared = ctx.enter_context(tc.tile_pool(name="shared", bufs=1))
        stage = ctx.enter_context(tc.tile_pool(name="stage", bufs=1))
        late = ctx.enter_context(tc.tile_pool(name="late", bufs=1))
        held = ctx.enter_context(tc.tile_pool(name="held", bufs=1))
        early = ctx.enter_context(tc.tile_pool(name="early", bufs=1))
        psum = ctx.enter_context(tc.psum_pool(name="psum", bufs=8))

        offs_sb = lists.tile([P, S // 16], U16, name="offs_sb")
        n1_sb = lists.tile([P, S // 16], U16, name="n1_sb")
        n2_sb = lists.tile([P, S // 16], U16, name="n2_sb")
        dst_sb = lists.tile([P, S // 16], U16, name="dst_sb")

        xs_table = sb.tile([P, T], U8, name="xs_table", align_bytes=64)
        w3s_raw = sb.tile([P, N], U8, name="w3s_raw", align_bytes=64)
        nc.vector.memset(xs_table[:].bitcast(I32), 0)
        nc.gpsimd.memset(w3s_raw[:].bitcast(I32), 0)


        nc.sync.dma_start(offs_sb[:], offs)
        nc.sync.dma_start(n1_sb[:], n1)
        nc.sync.dma_start(n2_sb[:], n2)
        w1_raw = [stage.tile([P, PACK, HALF], F32, name="w1_raw%d" % a, offset=a * RAW) for a in range(2)]
        w1_view = w1.rearrange("(p j) c -> p j c", j=PACK)
        for a in range(2):
            nc.sync.dma_start(out=w1_raw[a][:], in_=w1_view[:, :, a * HALF : (a + 1) * HALF])
        scale_rows_in(nc.scalar, xs_table, x_scales[0])
        scale_rows_in(nc.gpsimd, w3s_raw, w3_scales[0])
        ident = sb.tile([P, P], F32, name="ident")
        make_identity(nc, ident[:])
        xw_table = shared.tile([P, T], U32, name="xw_table", align_bytes=64, offset=0)
        nc.sync.dma_start(out=xw_table[:].bitcast(I32), in_=x_words[0].rearrange("p n t -> p (n t)").bitcast(I32))
        nc.sync.dma_start(dst_sb[:], dst)

        xs = sb.tile([P, S], U8, name="xs", align_bytes=64)
        nc.vector.tensor_copy(out=xs[:], in_=xs_table[:].indirect(offs_sb[:]))
        w1_bf = sb.tile([P, PACK * H], BF16, name="w1_bf", align_bytes=64)
        w1_dealt = w1_bf[:].rearrange("p (t m j) -> p m j t", t=PACK, j=PACK)
        for a in range(2):
            src = w1_raw[a][:].rearrange("p j (m t) -> p m j t", t=PACK)
            m0 = a * 64
            nc.vector.tensor_copy(out=w1_dealt[:, m0 : m0 + W_VEC], in_=src[:, 0:W_VEC])
            nc.scalar.activation(out=w1_dealt[:, m0 + W_VEC : m0 + 64], in_=src[:, W_VEC:64], func=ACT.Copy)
        w3w_raw = stage.tile([P, N], U32, name="w3w_raw", offset=0)
        nc.sync.dma_start(out=w3w_raw[:].bitcast(I32), in_=w3_words[0].rearrange("p n t -> p (n t)").bitcast(I32))
        w2_raw = stage.tile([P, PACK, H], F32, name="w2_raw", offset=RAW)
        nc.sync.dma_start(out=w2_raw[:], in_=w2.rearrange("(p j) c -> p j c", j=PACK))
        w1_q = sb.tile([P, H], U32, name="w1_q", align_bytes=64)
        w1_s = sb.tile([P, H], U8, name="w1_s", align_bytes=64)
        nc.vector.quantize_mx(out=w1_q[:].bitcast(FP8X4), scales=w1_s[:], in_=w1_bf[:])

        xw = [late.tile([P, HALF], U32, name="xw%d" % a, align_bytes=64, offset=a * 4 * HALF) for a in range(2)]
        for a in range(2):
            nc.vector.tensor_copy(out=xw[a][:], in_=xw_table[:].indirect(offs_sb[:, a * LIST_COLS : (a + 1) * LIST_COLS]))

        y_win = [sb.tile([P, S], F32, name="y_win%d" % t) for t in range(PACK)]
        y_neg = sb.tile([P, PACK, S], F32, name="y_neg")

        def first_layer(t, a):
            cols = slice(t * P, (t + 1) * P)
            half = slice(a * HALF, (a + 1) * HALF)
            bank = psum.tile([P, S], F32, name="bank", tag="bank")
            nc.tensor.matmul_mx(
                out=bank[:, 0:HALF], lhsT=w1_q[:, cols].bitcast(FP8X4), lhsT_scale=w1_s[:, cols],
                rhs=xw[a][:].bitcast(FP8X4), rhs_scale=xs[:, half], start=True, stop=True,
            )
            nc.scalar.copy(out=y_win[t][:, half], in_=bank[:, 0:HALF])
            if a == 0:
                nc.scalar.activation(out=y_neg[:, t, half], in_=bank[:, 0:HALF], func=ACT.Copy, scale=-1.0)

        for t in range(PACK):
            for a in range(2):
                first_layer(t, a)

        w3_q = shared.tile([P, N], U32, name="w3_q", align_bytes=64, offset=0)
        w3_s = shared.tile([P, N], U8, name="w3_s", align_bytes=64, offset=4 * N)
        nc.vector.tensor_copy(out=w3_q[:].rearrange("p (t m) -> p m t", t=PACK), in_=w3w_raw[:].rearrange("p (m t) -> p m t", t=PACK))
        nc.vector.tensor_copy(out=w3_s[:].rearrange("p (t m) -> p m t", t=PACK), in_=w3s_raw[:].rearrange("p (m t) -> p m t", t=PACK))

        w2_bf = late.tile([P, PACK * H], BF16, name="w2_bf", align_bytes=64, offset=0)
        w2_dealt = w2_bf[:].rearrange("p (t m j) -> p m j t", t=PACK, j=PACK)
        w2_src = w2_raw[:].rearrange("p j (m t) -> p m j t", t=PACK)
        w2_q = sb.tile([P, H], U32, name="w2_q", align_bytes=64)
        w2_s = sb.tile([P, H], U8, name="w2_s", align_bytes=64)

        second, gap, lift, sums, turned, z_bf, h_ps = {}, {}, {}, {}, {}, {}, {}
        hr = sb.tile([P, PACK, S], F32, name="hr")

        def negate(a):
            for t in range(PACK):
                half = slice(a * HALF, (a + 1) * HALF)
                nc.scalar.activation(out=y_neg[:, t, half], in_=y_win[t][:, half], func=ACT.Copy, scale=-1.0)

        def fetch_second(unit):
            a, t = divmod(unit, PACK)
            if unit >= 6:
                second[unit] = early.tile([P, HALF], F32, name="second%d" % unit, align_bytes=64, offset=(unit - 6) * 4 * HALF)
            else:
                second[unit] = sb.tile([P, HALF], F32, name="second%d" % unit)
            nc.vector.tensor_copy(out=second[unit][:], in_=y_win[t][:].indirect(n2_sb[:, a * LIST_COLS : (a + 1) * LIST_COLS]))

        def fetch_gap(unit):
            a, t = divmod(unit, PACK)
            gap[unit] = sb.tile([P, HALF], F32, name="gap%d" % unit)
            nc.vector.tensor_tensor(
                out=gap[unit][:], in0=y_win[t][:].indirect(n1_sb[:, a * LIST_COLS : (a + 1) * LIST_COLS]), in1=second[unit][:], op=ALU.subtract
            )

        def add_up(unit):
            a, t = divmod(unit, PACK)
            lift[unit] = sb.tile([P, HALF], F32, name="lift%d" % unit)
            nc.scalar.activation(out=lift[unit][:], in_=gap[unit][:], func=ACT.Relu)
            for i in range(2):
                b = 2 * a + i
                if t == 0:
                    sums[b] = psum.tile([P, S], F32, name="bank", tag="bank")
                part = slice(i * BLOCK, (i + 1) * BLOCK)
                terms = (y_neg[:, t, b * BLOCK : (b + 1) * BLOCK], second[unit][:, part], lift[unit][:, part])
                for n, term in enumerate(terms):
                    nc.tensor.matmul(sums[b][:, t * P : (t + 1) * P], lhsT=term, rhs=ident[:], is_transpose=True, start=(n == 0), stop=(n == 2))

        def turn_back(b):
            pairs = sb.tile([P, PACK * P], BF16, name="pairs%d" % b)
            nc.scalar.activation(
                out=pairs[:].rearrange("c (u p e) -> c u p e", u=2, e=2), in_=sums[b][:].rearrange("c (u e p) -> c u p e", u=2, e=2),
                func=ACT.Copy,
            )
            turned[b] = psum.tile([P, S], F32, name="bank", tag="bank")
            for u in range(2):
                nc.tensor.transpose(turned[b][:, u * BLOCK : (u + 1) * BLOCK], pairs[:].bitcast(F32)[:, u * P : (u + 1) * P], ident[:])

        def weave(b, tile, at):
            nc.scalar.copy(
                out=tile[:].bitcast(F32)[:, at * 2 * BLOCK : (at + 1) * 2 * BLOCK].rearrange("p (c u) -> p c u", u=2),
                in_=turned[b][:, 0 : 2 * BLOCK].rearrange("p (u c) -> p c u", u=2),
            )

        def second_layer(name, tile, width):
            z_q = sb.tile([P, width], U32, name="z_q%d" % name, align_bytes=64)
            z_s = sb.tile([P, width], U8, name="z_s%d" % name, align_bytes=64)
            nc.vector.quantize_mx(out=z_q[:].bitcast(FP8X4), scales=z_s[:], in_=tile[:])
            per_bank = S // width
            for t in range(PACK):
                if t % per_bank == 0:
                    bank = psum.tile([P, S], F32, name="bank", tag="bank")
                at = slice((t % per_bank) * width, (t % per_bank + 1) * width)
                cols = slice(t * P, (t + 1) * P)
                nc.tensor.matmul_mx(
                    out=bank[:, at], lhsT=w2_q[:, cols].bitcast(FP8X4), lhsT_scale=w2_s[:, cols],
                    rhs=z_q[:].bitcast(FP8X4), rhs_scale=z_s[:], start=True, stop=True,
                )
                h_ps[(name, t)] = (bank, t % per_bank)

        def relu_out(name, t0, count, c0, width):
            bank, at = h_ps[(name, t0)]
            nc.scalar.activation(
                out=hr[:, t0 : t0 + count, c0 : c0 + width],
                in_=bank[:, at * width : (at + count) * width].rearrange("p (t c) -> p t c", t=count), func=ACT.Relu, scale=-1.0,
            )

        hs = [sb.tile([P, S], F32, name="hs%d" % t) for t in range(PACK - 1)]
        z_bf[0] = early.tile([P, PACK * HALF], BF16, name="z_bf0", align_bytes=64, offset=0)
        z_bf[1] = held.tile([P, PACK * HALF], BF16, name="z_bf1", align_bytes=64, offset=0)

        def send(t, c0, width):
            nc.vector.tensor_copy(out=hs[t][:].indirect(dst_sb[:, c0 // 16 : (c0 + width) // 16]), in_=hr[:, t, c0 : c0 + width])

        d1 = sb.tile([P, PACK, HALF], F32, name="d1")
        d2 = sb.tile([P, PACK, HALF], F32, name="d2")
        for t in range(PACK):
            nc.vector.tensor_tensor(out=d1[:, t, :], in0=y_win[t][:].indirect(n1_sb[:, 0:LIST_COLS]), in1=y_neg[:, t, 0:HALF], op=ALU.add)
            nc.vector.tensor_tensor(out=d2[:, t, :], in0=y_win[t][:].indirect(n2_sb[:, 0:LIST_COLS]), in1=y_neg[:, t, 0:HALF], op=ALU.add)
        nc.scalar.activation(out=w2_dealt, in_=w2_src, func=ACT.Copy)
        negate(1)
        fetch_second(4)
        nc.vector.tensor_tensor(out=interleaved(z_bf[0][:]), in0=planes(d1[:]), in1=planes(d2[:]), op=ALU.max)
        fetch_second(5)
        nc.vector.quantize_mx(out=w2_q[:].bitcast(FP8X4), scales=w2_s[:], in_=w2_bf[:])
        second_layer(0, z_bf[0], HALF)
        for unit in range(PACK, 2 * PACK):
            if unit + 2 < 2 * PACK:
                fetch_second(unit + 2)
            fetch_gap(unit)
            add_up(unit)
            if unit % 2 == 0:
                relu_out(0, unit - PACK, 2, 0, HALF)
        turn_back(2)
        turn_back(3)
        weave(2, z_bf[1], 0)
        weave(3, z_bf[1], 1)
        for t in range(PACK - 1):
            send(t, 0, HALF)
        second_layer(1, z_bf[1], HALF)
        hs.append(held.tile([P, S], F32, name="hs3", align_bytes=64, offset=0))
        send(PACK - 1, 0, HALF)
        relu_out(1, 0, 2, HALF, HALF)
        relu_out(1, 2, 2, HALF, HALF)
        for t in range(PACK):
            send(t, HALF, HALF)

        hs_all = sb.tile([P, PACK, S], F32, name="hs_all")
        for t in range(PACK - 1):
            nc.scalar.copy(out=hs_all[:, t, :], in_=hs[t][:])
        for b in range(S // BLOCK):
            cols = slice(b * BLOCK, (b + 1) * BLOCK)
            nc.scalar.copy(out=hs_all[:, PACK - 1, cols], in_=hs[PACK - 1][:, cols])

        res_sb = stage.tile([P, PACK, S], F32, name="res_sb", offset=RAW)
        nc.sync.dma_start(out=res_sb[:], in_=res.rearrange("(p t) c -> p t c", t=PACK))
        out_view = out_0.rearrange("(p t) c -> p t c", t=PACK)
        words_view = out_1[0].rearrange("p n t -> p (n t)").bitcast(I32)
        o_q = sb.tile([P, S], U32, name="o_q", align_bytes=64)
        o_s = sb.tile([P, S], U8, name="o_s", align_bytes=64)
        nblocks = S // BLOCK
        z2_bf, banks, o_f = {}, {}, {}
        o_bf = sb.tile([P, PACK * S], BF16, name="o_bf", align_bytes=64)

        def subtract(b):
            cols = slice(b * BLOCK, (b + 1) * BLOCK)
            z2_bf[b] = sb.tile([P, PACK * BLOCK], BF16, name="z2_bf%d" % b, align_bytes=64)
            nc.vector.tensor_tensor(out=interleaved(z2_bf[b][:]), in0=planes(hs_all[:, :, cols]), in1=planes(y_neg[:, :, cols]), op=ALU.add)

        def multiply(b):
            z2_q = sb.tile([P, BLOCK], U32, name="z2_q%d" % b, align_bytes=64)
            z2_s = sb.tile([P, BLOCK], U8, name="z2_s%d" % b, align_bytes=64)
            nc.vector.quantize_mx(out=z2_q[:].bitcast(FP8X4), scales=z2_s[:], in_=z2_bf[b][:])
            banks[b] = psum.tile([P, S], F32, name="bank", tag="bank")
            for t in range(PACK):
                cols = slice(t * P, (t + 1) * P)
                nc.tensor.matmul_mx(
                    out=banks[b][:, t * BLOCK : (t + 1) * BLOCK], lhsT=w3_q[:, cols].bitcast(FP8X4), lhsT_scale=w3_s[:, cols],
                    rhs=z2_q[:].bitcast(FP8X4), rhs_scale=z2_s[:], start=True, stop=True,
                )

        def add_residual(b):
            cols = slice(b * BLOCK, (b + 1) * BLOCK)
            o_f[b] = sb.tile([P, PACK, BLOCK], F32, name="o_f%d" % b)
            nc.vector.tensor_tensor(out=o_f[b][:], in0=banks[b][:].rearrange("p (t c) -> p t c", t=PACK), in1=res_sb[:, :, cols], op=ALU.add)
            nc.sync.dma_start(out=out_view[:, :, cols], in_=o_f[b][:])
            nc.scalar.copy(out=interleaved(o_bf[:, PACK * b * BLOCK : PACK * (b + 1) * BLOCK]), in_=planes(o_f[b][:]))

        def hand_on(b0, b1):
            cols = slice(b0 * BLOCK, b1 * BLOCK)
            nc.vector.quantize_mx(out=o_q[:, cols].bitcast(FP8X4), scales=o_s[:, cols], in_=o_bf[:, PACK * b0 * BLOCK : PACK * b1 * BLOCK])
            nc.sync.dma_start(out=words_view[:, cols], in_=o_q[:, cols].bitcast(I32))

        for b in range(nblocks):
            subtract(b)
            if b >= 1:
                multiply(b - 1)
        add_residual(0)
        multiply(nblocks - 1)
        for b in range(1, nblocks):
            add_residual(b)
        hand_on(0, 2)
        hand_on(2, 3)
        hand_on(3, 4)
        for q in range(4):
            queue = nc.sync if q == 0 else nc.scalar
            queue.dma_start(out=out_2[0][4 * q : 4 * q + 4, :].bitcast(I32), in_=o_s[32 * q : 32 * q + 4, :].bitcast(I32))
